import numpy as np
import ml_dtypes


def mxq(x, axis, fmt="e4m3"):
    dtype, down = {"e4m3": (ml_dtypes.float8_e4m3fn, 7), "e5m2": (ml_dtypes.float8_e5m2, 14)}[fmt]
    v = np.moveaxis(np.asarray(x, np.float32).astype(ml_dtypes.bfloat16).astype(np.float64), axis, -1)
    blocks = v.reshape(v.shape[:-1] + (-1, 32))
    amax = np.abs(blocks).max(-1, keepdims=True)
    byte = np.maximum(np.where(amax > 0, np.frexp(amax)[1] - 1 + 127, 0) - down, 1)
    scale = np.exp2(byte - 127.0)
    codes = (blocks / scale).astype(np.float32).astype(dtype).astype(np.float64)
    return np.moveaxis((codes * scale).reshape(v.shape), -1, axis)


WIDE = False


def mx_kscale(k, group=512):
    if not WIDE:
        return np.ones(k)
    levels = np.array([10, -10, 5, -5, 0])
    if group != 512:
        return np.exp2(np.random.permutation(np.resize(levels, k // group))).repeat(group)
    if k % 512:
        return np.exp2(np.random.permutation(np.resize(levels, k // 32))).repeat(32)
    a = np.empty((k // 512, 16))
    for p in range(k // 512):
        a[p, :8] = np.random.permutation(np.resize(levels, 8))
        for g in range(8):
            far = levels[np.abs(levels - a[p, g]) >= 10]
            a[p, g + 8] = far[np.random.randint(len(far))]
    return np.exp2(a.ravel()).repeat(32)


def f64(x):
    return np.asarray(x).astype(np.float64)


def striped(idx):
    return np.tile(np.asarray(idx).reshape(-1, 16).T, (8, 1)).astype(np.uint16)


def unstriped(offs):
    return offs[:16].T.reshape(-1).astype(np.int64)


H, KV, D, NQ, N = 4, 4, 128, 512, 512
CAP = 2.0


def setup_inputs():
    n = np.random.standard_normal
    s = mx_kscale(D, 0)[:, None]
    u = mx_kscale(N)
    t = np.random.uniform(0.5, 2.0, N) * u
    v = n((KV, N, 128))
    v[:, :, 127] = 1.0
    return {
        "qT": (n((H, D, NQ)) * s * (0.70 / np.sqrt(D))).astype(np.float32),
        "kT": (n((KV, D, N)) / s).astype(np.float32),
        "t": t.reshape(N, 1).astype(np.float32),
        "v": (v / t[:, None]).astype(np.float32),
        "kb": (0.5 * n((N, 1))).astype(np.float32),
        "mask": (np.arange(N)[:, None] <= np.sort(np.random.randint(N // 4, N, NQ))[None, :]).astype(np.float32),
    }


def reference(qT, kT, t, v, kb, mask):
    a = mxq(f64(kT), 1, "e4m3").transpose(0, 2, 1) @ mxq(f64(qT), 1, "e4m3")
    a = a + f64(kb)
    a = CAP * np.tanh(a / CAP)
    p = np.exp(a)
    p = p * f64(mask)
    w = p * f64(t)
    y = mxq(w, 1, "e4m3").transpose(0, 2, 1) @ mxq(f64(v), 1, "e4m3")
    y = y / (y[:, :, 127:128])
    return y

@@ -1,0 +1,233 @@
+from contextlib import ExitStack
+
+import concourse.mybir as mybir
+
+H, D, NQ, N, E = 4, 128, 512, 512, 128
+CAP = 2.0
+FLOPS = 2 * H * N * NQ * D + 2 * H * NQ * N * E
+
+F32 = mybir.dt.float32
+BF16 = mybir.dt.bfloat16
+U32 = mybir.dt.uint32
+U8 = mybir.dt.uint8
+FP8X4 = mybir.dt.float8_e4m3fn_x4
+ACT = mybir.ActivationFunctionType
+ALU = mybir.AluOpType
+
+P = 128
+PACK = 4
+ROWS = D // PACK
+QT = 128
+HALF = NQ // 2
+UNITS = 2 * H
+
+
+def tile_rows_a_exp_kb_mask_cap_kernel(tc, qT, kT, t, v, kb, mask, out):
+    nc = tc.nc
+    with ExitStack() as ctx:
+        sb = ctx.enter_context(tc.tile_pool(name="sb", bufs=1))
+        ps = ctx.enter_context(tc.psum_pool(name="ps", bufs=1))
+        ctx.enter_context(tc.manual_schedule())
+
+        def mx_pair(name, words):
+            codes = sb.tile([P, words], U32, name=name + "_codes", align_bytes=64)
+            scales = sb.tile([P, words], U8, name=name + "_scales", align_bytes=64)
+            return codes, scales
+
+        def quantize(pair, src, w0, w1):
+            codes, scales = pair
+            nc.vector.quantize_mx(out=codes[:, w0:w1].bitcast(FP8X4), scales=scales[:, w0:w1],
+                                  in_=src[:, PACK * w0:PACK * w1])
+
+        kb_sb = sb.tile([P, PACK], F32, name="kb_sb")
+        t_sb = sb.tile([P, PACK], F32, name="t_sb")
+        nc.scalar.dma_start(out=kb_sb[:], in_=kb.rearrange("(p j) o -> p (j o)", j=PACK))
+        nc.scalar.dma_start(out=t_sb[:], in_=t.rearrange("(p j) o -> p (j o)", j=PACK))
+
+        k_raw = sb.tile([P, PACK, N], F32, name="k_raw")
+        nc.sync.dma_start(out=k_raw[:], in_=kT.rearrange("h (p j) n -> (h p) j n", j=PACK))
+        q_view = qT.rearrange("h (p j) q -> (h p) j q", j=PACK)
+        q_raw = [sb.tile([P, PACK, HALF], F32, name="q_raw%d" % a) for a in range(2)]
+        nc.sync.dma_start(out=q_raw[0][:], in_=q_view[:, :, 0:HALF])
+        mask_raw = sb.tile([P, PACK, NQ], F32, name="mask_raw")
+        nc.sync.dma_start(out=mask_raw[:], in_=mask.rearrange("(p j) q -> p j q", j=PACK))
+        v_view = v.rearrange("h (p j) e -> p h (j e)", j=PACK)
+        v_raw = [sb.tile([P, 2, PACK * E], F32, name="v_raw%d" % b) for b in range(2)]
+        nc.sync.dma_start(out=v_raw[0][:], in_=v_view[:, 0:2, :])
+        nc.sync.dma_start(out=q_raw[1][:], in_=q_view[:, :, HALF:NQ])
+        nc.sync.dma_start(out=v_raw[1][:], in_=v_view[:, 2:4, :])
+
+        kb_half = sb.tile([P, PACK], F32, name="kb_half")
+        k_bf = [sb.tile([P, 2 * P * PACK], BF16, name="k_bf%d" % u, align_bytes=64) for u in range(2)]
+        k_mx = [mx_pair("k%d" % u, 2 * P) for u in range(2)]
+        q_bf = [sb.tile([P, QT * PACK], BF16, name="q_bf%d" % g, align_bytes=64) for g in range(2)]
+        q_bf_b = sb.tile([P, HALF * PACK], BF16, name="q_bf_b", align_bytes=64)
+        q_mx_a = [mx_pair("qa%d" % g, QT) for g in range(2)]
+        q_mx_b = mx_pair("qb", HALF)
+        v_bf = [sb.tile([P, 2 * E * PACK], BF16, name="v_bf%d" % b, align_bytes=64) for b in range(2)]
+        v_mx = [mx_pair("v%d" % b, 2 * E) for b in range(2)]
+        mt = sb.tile([P, PACK, NQ], F32, name="mt")
+        th = [sb.tile([P, PACK, HALF], F32, name="th%d" % u) for u in range(UNITS)]
+        pw = [sb.tile([P, PACK, HALF], F32, name="pw%d" % u) for u in range(UNITS - 1)]
+        pw_last = [sb.tile([P, PACK, QT], F32, name="pw_last%d" % g) for g in range(2)]
+        w_bf = [sb.tile([P, HALF * PACK], BF16, name="w_bf%d" % u, align_bytes=64) for u in range(UNITS - 1)]
+        w_mx = [mx_pair("w%d" % u, HALF) for u in range(UNITS - 1)]
+        w_bf_last = [sb.tile([P, QT * PACK], BF16, name="w_bf_last%d" % g, align_bytes=64) for g in range(2)]
+        w_mx_last = [mx_pair("w_last%d" % g, QT) for g in range(2)]
+
+        score_banks = {}
+        for h in range(H):
+            for u in range(2):
+                if u == 0 or h in (0, H - 1):
+                    score_banks[h, u] = ps.tile([P, 2, HALF], F32, name="s_%d_%d" % (h, u))
+                else:
+                    score_banks[h, u] = score_banks[h, 0]
+        y_banks = [ps.tile([P, 4, E], F32, name="y%d" % b) for b in range(2)]
+
+        def copy_k(engine_copy, u):
+            engine_copy(out=k_bf[u][:].rearrange("p (r s j) -> p s j r", r=2, j=PACK),
+                        in_=k_raw[:].rearrange("p j (s r) -> p s j r", r=PACK)[:, :, :, 2 * u:2 * u + 2])
+
+        def copy_q(engine_copy, dst, src):
+            engine_copy(out=dst.rearrange("p (c i j) -> p c j i", i=4, j=PACK),
+                        in_=src.rearrange("p j (c i) -> p c j i", i=4))
+
+        def copy_v(b):
+            nc.vector.tensor_copy(out=v_bf[b][:].rearrange("p (h c i j) -> p h c j i", h=2, i=4, j=PACK),
+                                  in_=v_raw[b][:].rearrange("p h (j c i) -> p h c j i", j=PACK, i=4))
+
+        def scores(unit, u):
+            half, h = divmod(unit, H)
+            rows = slice(ROWS * h, ROWS * (h + 1))
+            kc, ks = k_mx[u]
+            for rr in range(2):
+                for g in range(2):
+                    if half == 0:
+                        qc, qs = q_mx_a[g]
+                        cols = slice(0, QT)
+                    else:
+                        qc, qs = q_mx_b
+                        cols = slice(QT * g, QT * (g + 1))
+                    nc.tensor.matmul_mx(out=score_banks[h, u][:, rr, QT * g:QT * (g + 1)],
+                                        lhsT=kc[rows, P * rr:P * (rr + 1)].bitcast(FP8X4),
+                                        lhsT_scale=ks[rows, P * rr:P * (rr + 1)],
+                                        rhs=qc[rows, cols].bitcast(FP8X4), rhs_scale=qs[rows, cols],
+                                        start=True, stop=True)
+
+        def cap(unit, r):
+            h = unit % H
+            nc.scalar.activation(out=th[unit][:, r, :], in_=score_banks[h, r // 2][:, r % 2, :], func=ACT.Tanh,
+                                 bias=kb_half[:, r:r + 1], scale=1.0 / CAP)
+
+        def weigh(dst, src):
+            nc.scalar.activation(out=dst, in_=src, func=ACT.Exp, scale=CAP)
+
+        def mask_scale(dst, src, q0, q1):
+            nc.vector.tensor_tensor(out=dst.rearrange("p (c i r) -> p c r i", i=2, r=PACK),
+                                    in0=src.rearrange("p r (c i) -> p c r i", i=2),
+                                    in1=mt[:, :, q0:q1].rearrange("p r (c i) -> p c r i", i=2), op=ALU.mult)
+
+        def values(pair, w0, h, dst):
+            wc, ws = pair
+            vc, vs = v_mx[h // 2]
+            cols = slice(E * (h % 2), E * (h % 2 + 1))
+            nc.tensor.matmul_mx(out=dst, lhsT=wc[:, w0:w0 + QT].bitcast(FP8X4), lhsT_scale=ws[:, w0:w0 + QT],
+                                rhs=vc[:, cols].bitcast(FP8X4), rhs_scale=vs[:, cols], start=True, stop=True)
+
+        def unit_values(unit):
+            for g in range(2):
+                values(w_mx[unit], QT * g, unit % H, y_banks[unit % 2][:, g, :])
+
+        def invert(name, bank, g0, g1):
+            rc = sb.tile([P, g1 - g0, 1], F32, name="rc_" + name)
+            nc.vector.reciprocal(out=rc[:], in_=bank[:, g0:g1, E - 1:E])
+            return rc
+
+        def store(queue, res, h, q0, groups):
+            queue.dma_start(out=out[h, q0:q0 + QT * groups, :].rearrange("(g p) e -> p g e", p=P), in_=res[:])
+
+        def divide_vector(name, bank, g0, g1, rc, h, q0):
+            res = sb.tile([P, g1 - g0, E], F32, name="res_" + name)
+            nc.vector.tensor_tensor(out=res[:], in0=bank[:, g0:g1, :], in1=rc[:].to_broadcast([P, g1 - g0, E]),
+                                    op=ALU.mult)
+            store(nc.sync, res, h, q0, g1 - g0)
+
+        def divide_scalar(name, bank, g0, g1, rc, h, q0):
+            res = sb.tile([P, g1 - g0, E], F32, name="res_" + name)
+            for g in range(g0, g1):
+                nc.scalar.activation(out=res[:, g - g0, :], in_=bank[:, g, :], func=ACT.Copy, scale=rc[:, g - g0, :])
+            store(nc.scalar, res, h, q0, g1 - g0)
+
+        nc.scalar.activation(out=kb_half[:], in_=kb_sb[:], func=ACT.Copy, scale=1.0 / CAP)
+        copy_k(nc.vector.tensor_copy, 0)
+        copy_k(nc.scalar.copy, 1)
+        quantize(k_mx[0], k_bf[0], 0, 2 * P)
+        copy_q(nc.vector.tensor_copy, q_bf[0][:], q_raw[0][:, :, 0:QT])
+        copy_q(nc.scalar.copy, q_bf[1][:], q_raw[0][:, :, QT:HALF])
+        quantize(k_mx[1], k_bf[1], 0, 2 * P)
+        quantize(q_mx_a[0], q_bf[0], 0, QT)
+        quantize(q_mx_a[1], q_bf[1], 0, QT)
+        scores(0, 0)
+        scores(0, 1)
+        for r in range(PACK):
+            nc.vector.tensor_scalar(out=mt[:, r, :], in0=mask_raw[:, r, :], scalar1=t_sb[:, r:r + 1], scalar2=None,
+                                    op0=ALU.mult)
+        copy_v(0)
+        for r in range(PACK):
+            cap(0, r)
+        scores(1, 0)
+
+        last = UNITS - 1
+        rcs = {}
+        for unit in range(1, UNITS):
+            prev = unit - 1
+            if unit < last:
+                scores(unit + 1, 0)
+                cap(unit, 0)
+                cap(unit, 1)
+                scores(unit, 1)
+                weigh(pw[prev][:], th[prev][:])
+                cap(unit, 2)
+                cap(unit, 3)
+            else:
+                scores(unit, 1)
+                cap(unit, 0)
+                weigh(pw[prev][:], th[prev][:])
+                cap(unit, 1)
+                cap(unit, 2)
+                cap(unit, 3)
+            if unit >= 2:
+                unit_values(unit - 2)
+                rcs[unit - 2] = invert("u%d" % (unit - 2), y_banks[unit % 2], 0, 2)
+            if unit == 2:
+                quantize(q_mx_b, q_bf_b, 0, HALF)
+            if unit == 3:
+                quantize(v_mx[1], v_bf[1], 0, 2 * E)
+            mask_scale(w_bf[prev][:], pw[prev][:], HALF * (prev // H), HALF * (prev // H + 1))
+            if unit == 1:
+                quantize(v_mx[0], v_bf[0], 0, 2 * E)
+            else:
+                u2 = unit - 2
+                divide_vector("u%d" % u2, y_banks[u2 % 2], 0, 2, rcs[u2], u2 % H, HALF * (u2 // H))
+            quantize(w_mx[prev], w_bf[prev], 0, HALF)
+            if unit == 1:
+                copy_q(nc.vector.tensor_copy, q_bf_b[:], q_raw[1][:])
+            if unit == 2:
+                copy_v(1)
+
+        h = last % H
+        prev = last - 1
+        for g in range(2):
+            weigh(pw_last[g][:], th[last][:, :, QT * g:QT * (g + 1)])
+        unit_values(prev)
+        mask_scale(w_bf_last[0][:], pw_last[0][:], HALF, HALF + QT)
+        rc_prev = invert("u%d" % prev, y_banks[prev % 2], 0, 2)
+        divide_scalar("u%d" % prev, y_banks[prev % 2], 0, 2, rc_prev, prev % H, HALF)
+        mask_scale(w_bf_last[1][:], pw_last[1][:], HALF + QT, NQ)
+        for g in range(2):
+            quantize(w_mx_last[g], w_bf_last[g], 0, QT)
+            values(w_mx_last[g], 0, h, y_banks[(last + g) % 2][:, 2, :])
+        rc0 = invert("last0", y_banks[last % 2], 2, 3)
+        rc1 = invert("last1", y_banks[(last + 1) % 2], 2, 3)
+        divide_scalar("last0", y_banks[last % 2], 2, 3, rc0, h, HALF)
+        divide_vector("last1", y_banks[(last + 1) % 2], 2, 3, rc1, h, HALF + QT)

@@ -20,6 +20,8 @@ ROWS = D // PACK
 QT = 128
 HALF = NQ // 2
 UNITS = 2 * H
+HEADS = (0, 1, 2, 3, 1, 2, 0, 3)
+TWO_BANKS = (0, 3)
 
 
 def tile_rows_a_exp_kb_mask_cap_kernel(tc, qT, kT, t, v, kb, mask, out):
@@ -44,11 +46,11 @@ def tile_rows_a_exp_kb_mask_cap_kernel(tc, qT, kT, t, v, kb, mask, out):
         nc.scalar.dma_start(out=kb_sb[:], in_=kb.rearrange("(p j) o -> p (j o)", j=PACK))
         nc.scalar.dma_start(out=t_sb[:], in_=t.rearrange("(p j) o -> p (j o)", j=PACK))
 
-        k_raw = sb.tile([P, PACK, N], F32, name="k_raw")
-        nc.sync.dma_start(out=k_raw[:], in_=kT.rearrange("h (p j) n -> (h p) j n", j=PACK))
         q_view = qT.rearrange("h (p j) q -> (h p) j q", j=PACK)
         q_raw = [sb.tile([P, PACK, HALF], F32, name="q_raw%d" % a) for a in range(2)]
         nc.sync.dma_start(out=q_raw[0][:], in_=q_view[:, :, 0:HALF])
+        k_raw = sb.tile([P, PACK, N], F32, name="k_raw")
+        nc.sync.dma_start(out=k_raw[:], in_=kT.rearrange("h (p j) n -> (h p) j n", j=PACK))
         mask_raw = sb.tile([P, PACK, NQ], F32, name="mask_raw")
         nc.sync.dma_start(out=mask_raw[:], in_=mask.rearrange("(p j) q -> p j q", j=PACK))
         v_view = v.rearrange("h (p j) e -> p h (j e)", j=PACK)
@@ -60,10 +62,8 @@ def tile_rows_a_exp_kb_mask_cap_kernel(tc, qT, kT, t, v, kb, mask, out):
         kb_half = sb.tile([P, PACK], F32, name="kb_half")
         k_bf = [sb.tile([P, 2 * P * PACK], BF16, name="k_bf%d" % u, align_bytes=64) for u in range(2)]
         k_mx = [mx_pair("k%d" % u, 2 * P) for u in range(2)]
-        q_bf = [sb.tile([P, QT * PACK], BF16, name="q_bf%d" % g, align_bytes=64) for g in range(2)]
-        q_bf_b = sb.tile([P, HALF * PACK], BF16, name="q_bf_b", align_bytes=64)
-        q_mx_a = [mx_pair("qa%d" % g, QT) for g in range(2)]
-        q_mx_b = mx_pair("qb", HALF)
+        q_bf = [sb.tile([P, HALF * PACK], BF16, name="q_bf%d" % a, align_bytes=64) for a in range(2)]
+        q_mx = [mx_pair("q%d" % a, HALF) for a in range(2)]
         v_bf = [sb.tile([P, 2 * E * PACK], BF16, name="v_bf%d" % b, align_bytes=64) for b in range(2)]
         v_mx = [mx_pair("v%d" % b, 2 * E) for b in range(2)]
         mt = sb.tile([P, PACK, NQ], F32, name="mt")
@@ -78,7 +78,7 @@ def tile_rows_a_exp_kb_mask_cap_kernel(tc, qT, kT, t, v, kb, mask, out):
         score_banks = {}
         for h in range(H):
             for u in range(2):
-                if u == 0 or h in (0, H - 1):
+                if u == 0 or h in TWO_BANKS:
                     score_banks[h, u] = ps.tile([P, 2, HALF], F32, name="s_%d_%d" % (h, u))
                 else:
                     score_banks[h, u] = score_banks[h, 0]
@@ -96,27 +96,28 @@ def tile_rows_a_exp_kb_mask_cap_kernel(tc, qT, kT, t, v, kb, mask, out):
             nc.vector.tensor_copy(out=v_bf[b][:].rearrange("p (h c i j) -> p h c j i", h=2, i=4, j=PACK),
                                   in_=v_raw[b][:].rearrange("p h (j c i) -> p h c j i", j=PACK, i=4))
 
+        def score_place(unit, r):
+            if unit == 0:
+                return score_banks[HEADS[unit], r % 2][:, 0, :]
+            return score_banks[HEADS[unit], r // 2][:, r % 2, :]
+
+        def scores_r(unit, r):
+            rows = slice(ROWS * HEADS[unit], ROWS * (HEADS[unit] + 1))
+            kc, ks = k_mx[r // 2]
+            kcols = slice(P * (r % 2), P * (r % 2 + 1))
+            qc, qs = q_mx[unit // H]
+            for g in range(2):
+                cols = slice(QT * g, QT * (g + 1))
+                nc.tensor.matmul_mx(out=score_place(unit, r)[:, cols], lhsT=kc[rows, kcols].bitcast(FP8X4),
+                                    lhsT_scale=ks[rows, kcols], rhs=qc[rows, cols].bitcast(FP8X4),
+                                    rhs_scale=qs[rows, cols], start=True, stop=True)
+
         def scores(unit, u):
-            half, h = divmod(unit, H)
-            rows = slice(ROWS * h, ROWS * (h + 1))
-            kc, ks = k_mx[u]
-            for rr in range(2):
-                for g in range(2):
-                    if half == 0:
-                        qc, qs = q_mx_a[g]
-                        cols = slice(0, QT)
-                    else:
-                        qc, qs = q_mx_b
-                        cols = slice(QT * g, QT * (g + 1))
-                    nc.tensor.matmul_mx(out=score_banks[h, u][:, rr, QT * g:QT * (g + 1)],
-                                        lhsT=kc[rows, P * rr:P * (rr + 1)].bitcast(FP8X4),
-                                        lhsT_scale=ks[rows, P * rr:P * (rr + 1)],
-                                        rhs=qc[rows, cols].bitcast(FP8X4), rhs_scale=qs[rows, cols],
-                                        start=True, stop=True)
+            scores_r(unit, 2 * u)
+            scores_r(unit, 2 * u + 1)
 
         def cap(unit, r):
-            h = unit % H
-            nc.scalar.activation(out=th[unit][:, r, :], in_=score_banks[h, r // 2][:, r % 2, :], func=ACT.Tanh,
+            nc.scalar.activation(out=th[unit][:, r, :], in_=score_place(unit, r), func=ACT.Tanh,
                                  bias=kb_half[:, r:r + 1], scale=1.0 / CAP)
 
         def weigh(dst, src):
@@ -136,7 +137,7 @@ def tile_rows_a_exp_kb_mask_cap_kernel(tc, qT, kT, t, v, kb, mask, out):
 
         def unit_values(unit):
             for g in range(2):
-                values(w_mx[unit], QT * g, unit % H, y_banks[unit % 2][:, g, :])
+                values(w_mx[unit], QT * g, HEADS[unit], y_banks[unit % 2][:, g, :])
 
         def invert(name, bank, g0, g1):
             rc = sb.tile([P, g1 - g0, 1], F32, name="rc_" + name)
@@ -152,82 +153,107 @@ def tile_rows_a_exp_kb_mask_cap_kernel(tc, qT, kT, t, v, kb, mask, out):
                                     op=ALU.mult)
             store(nc.sync, res, h, q0, g1 - g0)
 
-        def divide_scalar(name, bank, g0, g1, rc, h, q0):
+        def divide_scalar(name, bank, g0, g1, rc, h, q0, queue):
             res = sb.tile([P, g1 - g0, E], F32, name="res_" + name)
             for g in range(g0, g1):
                 nc.scalar.activation(out=res[:, g - g0, :], in_=bank[:, g, :], func=ACT.Copy, scale=rc[:, g - g0, :])
-            store(nc.scalar, res, h, q0, g1 - g0)
+            store(queue, res, h, q0, g1 - g0)
+
+        def invert_unit(unit):
+            return invert("u%d" % unit, y_banks[unit % 2], 0, 2)
+
+        def weigh_unit(unit):
+            weigh(pw[unit][:], th[unit][:])
+
+        def mask_unit(unit):
+            mask_scale(w_bf[unit][:], pw[unit][:], HALF * (unit // H), HALF * (unit // H + 1))
 
         nc.scalar.activation(out=kb_half[:], in_=kb_sb[:], func=ACT.Copy, scale=1.0 / CAP)
+        copy_q(nc.vector.tensor_copy, q_bf[0][:], q_raw[0][:])
+        quantize(q_mx[0], q_bf[0], 0, HALF)
         copy_k(nc.vector.tensor_copy, 0)
         copy_k(nc.scalar.copy, 1)
-        quantize(k_mx[0], k_bf[0], 0, 2 * P)
-        copy_q(nc.vector.tensor_copy, q_bf[0][:], q_raw[0][:, :, 0:QT])
-        copy_q(nc.scalar.copy, q_bf[1][:], q_raw[0][:, :, QT:HALF])
+        quantize(k_mx[0], k_bf[0], 0, P)
+        quantize(k_mx[0], k_bf[0], P, 2 * P)
         quantize(k_mx[1], k_bf[1], 0, 2 * P)
-        quantize(q_mx_a[0], q_bf[0], 0, QT)
-        quantize(q_mx_a[1], q_bf[1], 0, QT)
         scores(0, 0)
-        scores(0, 1)
+        scores(1, 0)
+        cap(0, 0)
+        scores_r(0, 2)
+        cap(0, 1)
+        scores_r(0, 3)
+        scores(2, 0)
         for r in range(PACK):
             nc.vector.tensor_scalar(out=mt[:, r, :], in0=mask_raw[:, r, :], scalar1=t_sb[:, r:r + 1], scalar2=None,
                                     op0=ALU.mult)
         copy_v(0)
-        for r in range(PACK):
-            cap(0, r)
-        scores(1, 0)
+        copy_q(nc.vector.tensor_copy, q_bf[1][:], q_raw[1][:])
+        quantize(v_mx[0], v_bf[0], 0, 2 * E)
+        cap(1, 0)
+        cap(1, 1)
+        scores(1, 1)
+        cap(0, 2)
+        cap(0, 3)
 
         last = UNITS - 1
-        rcs = {}
-        for unit in range(1, UNITS):
+        for unit in range(1, last - 1):
             prev = unit - 1
-            if unit < last:
-                scores(unit + 1, 0)
-                cap(unit, 0)
-                cap(unit, 1)
-                scores(unit, 1)
-                weigh(pw[prev][:], th[prev][:])
-                cap(unit, 2)
-                cap(unit, 3)
-            else:
-                scores(unit, 1)
-                cap(unit, 0)
-                weigh(pw[prev][:], th[prev][:])
-                cap(unit, 1)
-                cap(unit, 2)
-                cap(unit, 3)
+            scores(unit + 2, 0)
+            if HEADS[unit + 2] in TWO_BANKS:
+                scores(unit + 2, 1)
             if unit >= 2:
                 unit_values(unit - 2)
-                rcs[unit - 2] = invert("u%d" % (unit - 2), y_banks[unit % 2], 0, 2)
-            if unit == 2:
-                quantize(q_mx_b, q_bf_b, 0, HALF)
-            if unit == 3:
-                quantize(v_mx[1], v_bf[1], 0, 2 * E)
-            mask_scale(w_bf[prev][:], pw[prev][:], HALF * (prev // H), HALF * (prev // H + 1))
+            cap(unit + 1, 0)
+            weigh_unit(prev)
+            cap(unit + 1, 1)
+            if HEADS[unit + 1] not in TWO_BANKS:
+                scores(unit + 1, 1)
+            cap(unit, 2)
+            cap(unit, 3)
+            mask_unit(prev)
             if unit == 1:
-                quantize(v_mx[0], v_bf[0], 0, 2 * E)
+                quantize(q_mx[1], q_bf[1], 0, HALF)
             else:
-                u2 = unit - 2
-                divide_vector("u%d" % u2, y_banks[u2 % 2], 0, 2, rcs[u2], u2 % H, HALF * (u2 // H))
+                rc = invert_unit(unit - 2)
             quantize(w_mx[prev], w_bf[prev], 0, HALF)
             if unit == 1:
-                copy_q(nc.vector.tensor_copy, q_bf_b[:], q_raw[1][:])
-            if unit == 2:
                 copy_v(1)
+            else:
+                u2 = unit - 2
+                divide_vector("u%d" % u2, y_banks[u2 % 2], 0, 2, rc, HEADS[u2], HALF * (u2 // H))
+            if unit == 2:
+                quantize(v_mx[1], v_bf[1], 0, 2 * E)
 
-        h = last % H
-        prev = last - 1
+        h = HEADS[last]
+        unit_values(4)
+        cap(6, 2)
+        weigh_unit(5)
+        cap(6, 3)
+        mask_unit(5)
+        rc = invert_unit(4)
+        quantize(w_mx[5], w_bf[5], 0, HALF)
+        divide_vector("u4", y_banks[0], 0, 2, rc, HEADS[4], HALF)
+        unit_values(5)
+        cap(last, 0)
+        weigh_unit(6)
+        for r in range(1, PACK):
+            cap(last, r)
         for g in range(2):
             weigh(pw_last[g][:], th[last][:, :, QT * g:QT * (g + 1)])
-        unit_values(prev)
+        mask_unit(6)
+        rc5 = invert_unit(5)
+        quantize(w_mx[6], w_bf[6], 0, HALF)
+        unit_values(6)
+        divide_scalar("u5", y_banks[1], 0, 2, rc5, HEADS[5], HALF, nc.sync)
         mask_scale(w_bf_last[0][:], pw_last[0][:], HALF, HALF + QT)
-        rc_prev = invert("u%d" % prev, y_banks[prev % 2], 0, 2)
-        divide_scalar("u%d" % prev, y_banks[prev % 2], 0, 2, rc_prev, prev % H, HALF)
         mask_scale(w_bf_last[1][:], pw_last[1][:], HALF + QT, NQ)
-        for g in range(2):
-            quantize(w_mx_last[g], w_bf_last[g], 0, QT)
-            values(w_mx_last[g], 0, h, y_banks[(last + g) % 2][:, 2, :])
-        rc0 = invert("last0", y_banks[last % 2], 2, 3)
-        rc1 = invert("last1", y_banks[(last + 1) % 2], 2, 3)
-        divide_scalar("last0", y_banks[last % 2], 2, 3, rc0, h, HALF)
-        divide_vector("last1", y_banks[(last + 1) % 2], 2, 3, rc1, h, HALF + QT)
+        rc6 = invert_unit(6)
+        divide_scalar("u6", y_banks[0], 0, 2, rc6, HEADS[6], HALF, nc.sync)
+        quantize(w_mx_last[0], w_bf_last[0], 0, QT)
+        values(w_mx_last[0], 0, h, y_banks[1][:, 2, :])
+        quantize(w_mx_last[1], w_bf_last[1], 0, QT)
+        values(w_mx_last[1], 0, h, y_banks[0][:, 2, :])
+        rc0 = invert("last0", y_banks[1], 2, 3)
+        rc1 = invert("last1", y_banks[0], 2, 3)
+        divide_scalar("last0", y_banks[1], 2, 3, rc0, h, HALF, nc.scalar)
+        divide_vector("last1", y_banks[0], 2, 3, rc1, h, HALF + QT)

@@ -19,9 +19,13 @@ PACK = 4
 ROWS = D // PACK
 QT = 128
 HALF = NQ // 2
-UNITS = 2 * H
-HEADS = (0, 1, 2, 3, 1, 2, 0, 3)
+BANK = 512
+RUN = 2
+
+JOBS = ((0, 0, 2), (1, 0, 2), (2, 0, 2), (3, 0, 4), (1, 2, 2), (2, 2, 2), (0, 2, 2))
+ROUNDS = ((0, 1, 2, 3), (4, 5), (6,))
 TWO_BANKS = (0, 3)
+EXP_LAG, SECOND_EXP_LAG = 1, 3
 
 
 def tile_rows_a_exp_kb_mask_cap_kernel(tc, qT, kT, t, v, kb, mask, out):
@@ -31,229 +35,232 @@ def tile_rows_a_exp_kb_mask_cap_kernel(tc, qT, kT, t, v, kb, mask, out):
         ps = ctx.enter_context(tc.psum_pool(name="ps", bufs=1))
         ctx.enter_context(tc.manual_schedule())
 
-        def mx_pair(name, words):
+        kb_sb = sb.tile([P, PACK], F32, name="kb_sb")
+        t_sb = sb.tile([P, PACK], F32, name="t_sb")
+        nc.scalar.dma_start(out=kb_sb[:], in_=kb.rearrange("(s r) o -> s (r o)", r=PACK))
+        nc.scalar.dma_start(out=t_sb[:], in_=t.rearrange("(s r) o -> s (r o)", r=PACK))
+
+        q_view = qT.rearrange("h (p j) q -> (h p) j q", j=PACK)
+        v_view = v.rearrange("h (s r) e -> s h (r e)", r=PACK)
+        q_raw = [sb.tile([P, PACK, HALF], F32, name="q_raw%d" % half) for half in range(2)]
+        k_raw = sb.tile([P, PACK, N], F32, name="k_raw")
+        mask_raw = sb.tile([P, PACK, NQ], F32, name="mask_raw")
+        v_raw = [sb.tile([P, 2, PACK * E], F32, name="v_raw%d" % pair) for pair in range(2)]
+        nc.sync.dma_start(out=q_raw[0][:], in_=q_view[:, :, 0:HALF])
+        nc.sync.dma_start(out=k_raw[:], in_=kT.rearrange("h (p j) n -> (h p) j n", j=PACK))
+        nc.sync.dma_start(out=mask_raw[:], in_=mask.rearrange("(s r) q -> s r q", r=PACK))
+        nc.sync.dma_start(out=q_raw[1][:], in_=q_view[:, :, HALF:NQ])
+        for pair in range(2):
+            nc.sync.dma_start(out=v_raw[pair][:], in_=v_view[:, 2 * pair:2 * pair + 2, :])
+
+        def rounded(name, words):
+            return sb.tile([P, PACK * words], BF16, name=name + "_bf", align_bytes=64)
+
+        def operand(name, words):
             codes = sb.tile([P, words], U32, name=name + "_codes", align_bytes=64)
             scales = sb.tile([P, words], U8, name=name + "_scales", align_bytes=64)
             return codes, scales
 
-        def quantize(pair, src, w0, w1):
-            codes, scales = pair
-            nc.vector.quantize_mx(out=codes[:, w0:w1].bitcast(FP8X4), scales=scales[:, w0:w1],
-                                  in_=src[:, PACK * w0:PACK * w1])
+        def quantize(dst, src, first, stop):
+            codes, scales = dst
+            nc.vector.quantize_mx(out=codes[:, first:stop].bitcast(FP8X4), scales=scales[:, first:stop],
+                                  in_=src[:, PACK * first:PACK * stop])
 
-        kb_sb = sb.tile([P, PACK], F32, name="kb_sb")
-        t_sb = sb.tile([P, PACK], F32, name="t_sb")
-        nc.scalar.dma_start(out=kb_sb[:], in_=kb.rearrange("(p j) o -> p (j o)", j=PACK))
-        nc.scalar.dma_start(out=t_sb[:], in_=t.rearrange("(p j) o -> p (j o)", j=PACK))
-
-        q_view = qT.rearrange("h (p j) q -> (h p) j q", j=PACK)
-        q_raw = [sb.tile([P, PACK, HALF], F32, name="q_raw%d" % a) for a in range(2)]
-        nc.sync.dma_start(out=q_raw[0][:], in_=q_view[:, :, 0:HALF])
-        k_raw = sb.tile([P, PACK, N], F32, name="k_raw")
-        nc.sync.dma_start(out=k_raw[:], in_=kT.rearrange("h (p j) n -> (h p) j n", j=PACK))
-        mask_raw = sb.tile([P, PACK, NQ], F32, name="mask_raw")
-        nc.sync.dma_start(out=mask_raw[:], in_=mask.rearrange("(p j) q -> p j q", j=PACK))
-        v_view = v.rearrange("h (p j) e -> p h (j e)", j=PACK)
-        v_raw = [sb.tile([P, 2, PACK * E], F32, name="v_raw%d" % b) for b in range(2)]
-        nc.sync.dma_start(out=v_raw[0][:], in_=v_view[:, 0:2, :])
-        nc.sync.dma_start(out=q_raw[1][:], in_=q_view[:, :, HALF:NQ])
-        nc.sync.dma_start(out=v_raw[1][:], in_=v_view[:, 2:4, :])
-
-        kb_half = sb.tile([P, PACK], F32, name="kb_half")
-        k_bf = [sb.tile([P, 2 * P * PACK], BF16, name="k_bf%d" % u, align_bytes=64) for u in range(2)]
-        k_mx = [mx_pair("k%d" % u, 2 * P) for u in range(2)]
-        q_bf = [sb.tile([P, HALF * PACK], BF16, name="q_bf%d" % a, align_bytes=64) for a in range(2)]
-        q_mx = [mx_pair("q%d" % a, HALF) for a in range(2)]
-        v_bf = [sb.tile([P, 2 * E * PACK], BF16, name="v_bf%d" % b, align_bytes=64) for b in range(2)]
-        v_mx = [mx_pair("v%d" % b, 2 * E) for b in range(2)]
-        mt = sb.tile([P, PACK, NQ], F32, name="mt")
-        th = [sb.tile([P, PACK, HALF], F32, name="th%d" % u) for u in range(UNITS)]
-        pw = [sb.tile([P, PACK, HALF], F32, name="pw%d" % u) for u in range(UNITS - 1)]
-        pw_last = [sb.tile([P, PACK, QT], F32, name="pw_last%d" % g) for g in range(2)]
-        w_bf = [sb.tile([P, HALF * PACK], BF16, name="w_bf%d" % u, align_bytes=64) for u in range(UNITS - 1)]
-        w_mx = [mx_pair("w%d" % u, HALF) for u in range(UNITS - 1)]
-        w_bf_last = [sb.tile([P, QT * PACK], BF16, name="w_bf_last%d" % g, align_bytes=64) for g in range(2)]
-        w_mx_last = [mx_pair("w_last%d" % g, QT) for g in range(2)]
+        q_bf = [rounded("q%d" % half, HALF) for half in range(2)]
+        q_mx = [operand("q%d" % half, HALF) for half in range(2)]
+        k_bf = [rounded("k%d" % pair, 2 * P) for pair in range(2)]
+        k_mx = [operand("k%d" % pair, 2 * P) for pair in range(2)]
+        v_bf = [rounded("v%d" % pair, 2 * E) for pair in range(2)]
+        v_mx = [operand("v%d" % pair, 2 * E) for pair in range(2)]
+        kb_scaled = sb.tile([P, PACK], F32, name="kb_scaled")
+        mask_t = sb.tile([P, PACK, NQ], F32, name="mask_t")
+        capped = [sb.tile([P, PACK, QT * job[2]], F32, name="capped%d" % n) for n, job in enumerate(JOBS)]
 
         score_banks = {}
         for h in range(H):
-            for u in range(2):
-                if u == 0 or h in TWO_BANKS:
-                    score_banks[h, u] = ps.tile([P, 2, HALF], F32, name="s_%d_%d" % (h, u))
-                else:
-                    score_banks[h, u] = score_banks[h, 0]
-        y_banks = [ps.tile([P, 4, E], F32, name="y%d" % b) for b in range(2)]
+            for b in range(2 if h in TWO_BANKS else 1):
+                score_banks[h, b] = ps.tile([P, BANK], F32, name="s_%d_%d" % (h, b))
+        y_banks = [ps.tile([P, 2, E], F32, name="y%d" % b) for b in range(2)]
 
-        def copy_k(engine_copy, u):
-            engine_copy(out=k_bf[u][:].rearrange("p (r s j) -> p s j r", r=2, j=PACK),
-                        in_=k_raw[:].rearrange("p j (s r) -> p s j r", r=PACK)[:, :, :, 2 * u:2 * u + 2])
+        def round_q(half):
+            nc.vector.tensor_copy(out=q_bf[half][:].rearrange("p (c i j) -> p c j i", i=RUN, j=PACK),
+                                  in_=q_raw[half][:].rearrange("p j (c i) -> p c j i", i=RUN))
 
-        def copy_q(engine_copy, dst, src):
-            engine_copy(out=dst.rearrange("p (c i j) -> p c j i", i=4, j=PACK),
-                        in_=src.rearrange("p j (c i) -> p c j i", i=4))
+        def round_k(copy, pair):
+            copy(out=k_bf[pair][:].rearrange("p (r s j) -> p s j r", r=2, j=PACK),
+                 in_=k_raw[:].rearrange("p j (s r) -> p s j r", r=PACK)[:, :, :, 2 * pair:2 * pair + 2])
 
-        def copy_v(b):
-            nc.vector.tensor_copy(out=v_bf[b][:].rearrange("p (h c i j) -> p h c j i", h=2, i=4, j=PACK),
-                                  in_=v_raw[b][:].rearrange("p h (j c i) -> p h c j i", j=PACK, i=4))
+        def round_v(pair):
+            nc.vector.tensor_copy(out=v_bf[pair][:].rearrange("s (h c i r) -> s h c r i", h=2, i=RUN, r=PACK),
+                                  in_=v_raw[pair][:].rearrange("s h (r c i) -> s h c r i", r=PACK, i=RUN))
 
-        def score_place(unit, r):
-            if unit == 0:
-                return score_banks[HEADS[unit], r % 2][:, 0, :]
-            return score_banks[HEADS[unit], r // 2][:, r % 2, :]
+        def bank_a_place(job):
+            return job == 0 or QT * JOBS[job][2] == BANK
 
-        def scores_r(unit, r):
-            rows = slice(ROWS * HEADS[unit], ROWS * (HEADS[unit] + 1))
-            kc, ks = k_mx[r // 2]
-            kcols = slice(P * (r % 2), P * (r % 2 + 1))
-            qc, qs = q_mx[unit // H]
-            for g in range(2):
-                cols = slice(QT * g, QT * (g + 1))
-                nc.tensor.matmul_mx(out=score_place(unit, r)[:, cols], lhsT=kc[rows, kcols].bitcast(FP8X4),
-                                    lhsT_scale=ks[rows, kcols], rhs=qc[rows, cols].bitcast(FP8X4),
-                                    rhs_scale=qs[rows, cols], start=True, stop=True)
+        def score_bank(job, r):
+            h = JOBS[job][0]
+            if bank_a_place(job):
+                return h, r % 2
+            return h, r // 2 if h in TWO_BANKS else 0
 
-        def scores(unit, u):
-            scores_r(unit, 2 * u)
-            scores_r(unit, 2 * u + 1)
+        def score_view(job, r):
+            width = QT * JOBS[job][2]
+            first = 0 if bank_a_place(job) else width * (r % 2)
+            return score_banks[score_bank(job, r)][:, first:first + width]
 
-        def cap(unit, r):
-            nc.scalar.activation(out=th[unit][:, r, :], in_=score_place(unit, r), func=ACT.Tanh,
-                                 bias=kb_half[:, r:r + 1], scale=1.0 / CAP)
+        def scores(job, r):
+            h, first_tile, tiles = JOBS[job]
+            rows = slice(ROWS * h, ROWS * (h + 1))
+            k_codes, k_scales = k_mx[r // 2]
+            tokens = slice(P * (r % 2), P * (r % 2 + 1))
+            for g in range(tiles):
+                half, tile_in_half = divmod(first_tile + g, 2)
+                q_codes, q_scales = q_mx[half]
+                queries = slice(QT * tile_in_half, QT * (tile_in_half + 1))
+                nc.tensor.matmul_mx(out=score_view(job, r)[:, QT * g:QT * (g + 1)],
+                                    lhsT=k_codes[rows, tokens].bitcast(FP8X4), lhsT_scale=k_scales[rows, tokens],
+                                    rhs=q_codes[rows, queries].bitcast(FP8X4), rhs_scale=q_scales[rows, queries],
+                                    start=True, stop=True)
 
-        def weigh(dst, src):
-            nc.scalar.activation(out=dst, in_=src, func=ACT.Exp, scale=CAP)
+        def cap(job, r):
+            nc.scalar.activation(out=capped[job][:, r, :], in_=score_view(job, r), func=ACT.Tanh,
+                                 bias=kb_scaled[:, r:r + 1], scale=1.0 / CAP)
 
-        def mask_scale(dst, src, q0, q1):
-            nc.vector.tensor_tensor(out=dst.rearrange("p (c i r) -> p c r i", i=2, r=PACK),
-                                    in0=src.rearrange("p r (c i) -> p c r i", i=2),
-                                    in1=mt[:, :, q0:q1].rearrange("p r (c i) -> p c r i", i=2), op=ALU.mult)
+        weights, w_bf, w_mx, inverse = {}, {}, {}, {}
 
-        def values(pair, w0, h, dst):
-            wc, ws = pair
-            vc, vs = v_mx[h // 2]
-            cols = slice(E * (h % 2), E * (h % 2 + 1))
-            nc.tensor.matmul_mx(out=dst, lhsT=wc[:, w0:w0 + QT].bitcast(FP8X4), lhsT_scale=ws[:, w0:w0 + QT],
-                                rhs=vc[:, cols].bitcast(FP8X4), rhs_scale=vs[:, cols], start=True, stop=True)
+        def weigh(chunk):
+            job, a, b = chunk
+            weights[chunk] = sb.tile([P, PACK, QT * (b - a)], F32, name="weights%d_%d" % (job, a))
+            nc.scalar.activation(out=weights[chunk][:], in_=capped[job][:, :, QT * a:QT * b], func=ACT.Exp, scale=CAP)
 
-        def unit_values(unit):
-            for g in range(2):
-                values(w_mx[unit], QT * g, HEADS[unit], y_banks[unit % 2][:, g, :])
+        def mask_and_round(chunk):
+            job, a, b = chunk
+            first_tile = JOBS[job][1]
+            factors = mask_t[:, :, QT * (first_tile + a):QT * (first_tile + b)]
+            w_bf[chunk] = rounded("w%d_%d" % (job, a), QT * (b - a))
+            nc.vector.tensor_tensor(out=w_bf[chunk][:].rearrange("s (c i r) -> s c r i", i=RUN, r=PACK),
+                                    in0=weights[chunk][:].rearrange("s r (c i) -> s c r i", i=RUN),
+                                    in1=factors.rearrange("s r (c i) -> s c r i", i=RUN), op=ALU.mult)
 
-        def invert(name, bank, g0, g1):
-            rc = sb.tile([P, g1 - g0, 1], F32, name="rc_" + name)
-            nc.vector.reciprocal(out=rc[:], in_=bank[:, g0:g1, E - 1:E])
-            return rc
+        def values(chunk, bank):
+            job, a, b = chunk
+            w_mx[chunk] = operand("w%d_%d" % (job, a), QT * (b - a))
+            quantize(w_mx[chunk], w_bf[chunk], 0, QT * (b - a))
+            pair, head_in_pair = divmod(JOBS[job][0], 2)
+            w_codes, w_scales = w_mx[chunk]
+            v_codes, v_scales = v_mx[pair]
+            features = slice(E * head_in_pair, E * (head_in_pair + 1))
+            for g in range(b - a):
+                queries = slice(QT * g, QT * (g + 1))
+                nc.tensor.matmul_mx(out=bank[:, g, :],
+                                    lhsT=w_codes[:, queries].bitcast(FP8X4), lhsT_scale=w_scales[:, queries],
+                                    rhs=v_codes[:, features].bitcast(FP8X4), rhs_scale=v_scales[:, features],
+                                    start=True, stop=True)
 
-        def store(queue, res, h, q0, groups):
-            queue.dma_start(out=out[h, q0:q0 + QT * groups, :].rearrange("(g p) e -> p g e", p=P), in_=res[:])
+        def invert(chunk, bank):
+            job, a, b = chunk
+            inverse[chunk] = sb.tile([P, b - a, 1], F32, name="inverse%d_%d" % (job, a))
+            nc.vector.reciprocal(out=inverse[chunk][:], in_=bank[:, 0:b - a, E - 1:E])
 
-        def divide_vector(name, bank, g0, g1, rc, h, q0):
-            res = sb.tile([P, g1 - g0, E], F32, name="res_" + name)
-            nc.vector.tensor_tensor(out=res[:], in0=bank[:, g0:g1, :], in1=rc[:].to_broadcast([P, g1 - g0, E]),
-                                    op=ALU.mult)
-            store(nc.sync, res, h, q0, g1 - g0)
+        def store(chunk, result, queue):
+            job, a, b = chunk
+            h, first_tile = JOBS[job][0:2]
+            rows = out[h, QT * (first_tile + a):QT * (first_tile + b), :]
+            queue.dma_start(out=rows.rearrange("(g p) e -> p g e", p=P), in_=result[:])
 
-        def divide_scalar(name, bank, g0, g1, rc, h, q0, queue):
-            res = sb.tile([P, g1 - g0, E], F32, name="res_" + name)
-            for g in range(g0, g1):
-                nc.scalar.activation(out=res[:, g - g0, :], in_=bank[:, g, :], func=ACT.Copy, scale=rc[:, g - g0, :])
-            store(queue, res, h, q0, g1 - g0)
+        def divide_on_vector(chunk, bank):
+            job, a, b = chunk
+            result = sb.tile([P, b - a, E], F32, name="result%d_%d" % (job, a))
+            nc.vector.tensor_tensor(out=result[:], in0=bank[:, 0:b - a, :],
+                                    in1=inverse[chunk][:].to_broadcast([P, b - a, E]), op=ALU.mult)
+            store(chunk, result, nc.sync)
 
-        def invert_unit(unit):
-            return invert("u%d" % unit, y_banks[unit % 2], 0, 2)
+        def divide_on_scalar(chunk, bank, queue):
+            job, a, b = chunk
+            result = sb.tile([P, b - a, E], F32, name="result%d_%d" % (job, a))
+            for g in range(b - a):
+                nc.scalar.activation(out=result[:, g, :], in_=bank[:, g, :], func=ACT.Copy,
+                                     scale=inverse[chunk][:, g, :])
+            store(chunk, result, queue)
 
-        def weigh_unit(unit):
-            weigh(pw[unit][:], th[unit][:])
-
-        def mask_unit(unit):
-            mask_scale(w_bf[unit][:], pw[unit][:], HALF * (unit // H), HALF * (unit // H + 1))
-
-        nc.scalar.activation(out=kb_half[:], in_=kb_sb[:], func=ACT.Copy, scale=1.0 / CAP)
-        copy_q(nc.vector.tensor_copy, q_bf[0][:], q_raw[0][:])
+        nc.scalar.activation(out=kb_scaled[:], in_=kb_sb[:], func=ACT.Copy, scale=1.0 / CAP)
+        round_q(0)
         quantize(q_mx[0], q_bf[0], 0, HALF)
-        copy_k(nc.vector.tensor_copy, 0)
-        copy_k(nc.scalar.copy, 1)
+        round_k(nc.vector.tensor_copy, 0)
+        round_k(nc.scalar.copy, 1)
         quantize(k_mx[0], k_bf[0], 0, P)
         quantize(k_mx[0], k_bf[0], P, 2 * P)
         quantize(k_mx[1], k_bf[1], 0, 2 * P)
-        scores(0, 0)
-        scores(1, 0)
-        cap(0, 0)
-        scores_r(0, 2)
-        cap(0, 1)
-        scores_r(0, 3)
-        scores(2, 0)
         for r in range(PACK):
-            nc.vector.tensor_scalar(out=mt[:, r, :], in0=mask_raw[:, r, :], scalar1=t_sb[:, r:r + 1], scalar2=None,
-                                    op0=ALU.mult)
-        copy_v(0)
-        copy_q(nc.vector.tensor_copy, q_bf[1][:], q_raw[1][:])
+            nc.vector.tensor_scalar(out=mask_t[:, r, :], in0=mask_raw[:, r, :], scalar1=t_sb[:, r:r + 1],
+                                    scalar2=None, op0=ALU.mult)
+        round_q(1)
+        quantize(q_mx[1], q_bf[1], 0, HALF)
+        round_v(0)
         quantize(v_mx[0], v_bf[0], 0, 2 * E)
-        cap(1, 0)
-        cap(1, 1)
-        scores(1, 1)
-        cap(0, 2)
-        cap(0, 3)
 
-        last = UNITS - 1
-        for unit in range(1, last - 1):
-            prev = unit - 1
-            scores(unit + 2, 0)
-            if HEADS[unit + 2] in TWO_BANKS:
-                scores(unit + 2, 1)
-            if unit >= 2:
-                unit_values(unit - 2)
-            cap(unit + 1, 0)
-            weigh_unit(prev)
-            cap(unit + 1, 1)
-            if HEADS[unit + 1] not in TWO_BANKS:
-                scores(unit + 1, 1)
-            cap(unit, 2)
-            cap(unit, 3)
-            mask_unit(prev)
-            if unit == 1:
-                quantize(q_mx[1], q_bf[1], 0, HALF)
-            else:
-                rc = invert_unit(unit - 2)
-            quantize(w_mx[prev], w_bf[prev], 0, HALF)
-            if unit == 1:
-                copy_v(1)
-            else:
-                u2 = unit - 2
-                divide_vector("u%d" % u2, y_banks[u2 % 2], 0, 2, rc, HEADS[u2], HALF * (u2 // H))
-            if unit == 2:
+        caps = []
+        for jobs in ROUNDS:
+            caps.extend([(jobs[0], 0), (jobs[0], 1)])
+            for before, job in zip(jobs, jobs[1:]):
+                caps.extend([(job, 0), (job, 1), (before, 2), (before, 3)])
+            caps.extend([(jobs[-1], 2), (jobs[-1], 3)])
+
+        fills = []
+        for job, r in caps:
+            if bank_a_place(job):
+                fills.append((job, (r,)))
+            elif r % 2 == 0:
+                fills.append((job, (r, r + 1)))
+        unread = {}
+
+        def fill_free_banks():
+            while fills and not unread.get(score_bank(fills[0][0], fills[0][1][0])):
+                job, places = fills.pop(0)
+                unread[score_bank(job, places[0])] = len(places)
+                for r in places:
+                    scores(job, r)
+
+        def run_caps(first, stop):
+            for job, r in caps[first:stop]:
+                cap(job, r)
+                unread[score_bank(job, r)] -= 1
+                fill_free_banks()
+
+        last_job = len(JOBS) - 1
+        chunks = [(job, a, a + 2) for job in range(last_job) for a in range(0, JOBS[job][2], 2)]
+        exp_at = [caps.index((job, PACK - 1)) + 1 + EXP_LAG + (SECOND_EXP_LAG if a else 0) for job, a, b in chunks]
+        exp_at.append(len(caps))
+
+        fill_free_banks()
+        run_caps(0, exp_at[0])
+        for n, chunk in enumerate(chunks):
+            weigh(chunk)
+            run_caps(exp_at[n], exp_at[n + 1])
+            mask_and_round(chunk)
+            if n == 0:
+                round_v(1)
+                values(chunk, y_banks[0])
                 quantize(v_mx[1], v_bf[1], 0, 2 * E)
+            else:
+                invert(chunks[n - 1], y_banks[(n - 1) % 2])
+                values(chunk, y_banks[n % 2])
+                if n + 1 < len(chunks):
+                    divide_on_vector(chunks[n - 1], y_banks[(n - 1) % 2])
 
-        h = HEADS[last]
-        unit_values(4)
-        cap(6, 2)
-        weigh_unit(5)
-        cap(6, 3)
-        mask_unit(5)
-        rc = invert_unit(4)
-        quantize(w_mx[5], w_bf[5], 0, HALF)
-        divide_vector("u4", y_banks[0], 0, 2, rc, HEADS[4], HALF)
-        unit_values(5)
-        cap(last, 0)
-        weigh_unit(6)
-        for r in range(1, PACK):
-            cap(last, r)
-        for g in range(2):
-            weigh(pw_last[g][:], th[last][:, :, QT * g:QT * (g + 1)])
-        mask_unit(6)
-        rc5 = invert_unit(5)
-        quantize(w_mx[6], w_bf[6], 0, HALF)
-        unit_values(6)
-        divide_scalar("u5", y_banks[1], 0, 2, rc5, HEADS[5], HALF, nc.sync)
-        mask_scale(w_bf_last[0][:], pw_last[0][:], HALF, HALF + QT)
-        mask_scale(w_bf_last[1][:], pw_last[1][:], HALF + QT, NQ)
-        rc6 = invert_unit(6)
-        divide_scalar("u6", y_banks[0], 0, 2, rc6, HEADS[6], HALF, nc.sync)
-        quantize(w_mx_last[0], w_bf_last[0], 0, QT)
-        values(w_mx_last[0], 0, h, y_banks[1][:, 2, :])
-        quantize(w_mx_last[1], w_bf_last[1], 0, QT)
-        values(w_mx_last[1], 0, h, y_banks[0][:, 2, :])
-        rc0 = invert("last0", y_banks[1], 2, 3)
-        rc1 = invert("last1", y_banks[0], 2, 3)
-        divide_scalar("last0", y_banks[1], 2, 3, rc0, h, HALF, nc.scalar)
-        divide_vector("last1", y_banks[0], 2, 3, rc1, h, HALF + QT)
+        second_last, newest = chunks[-2], chunks[-1]
+        banks = [y_banks[len(chunks) % 2], y_banks[(len(chunks) + 1) % 2]]
+        ends = [(last_job, g, g + 1) for g in range(2)]
+        for end in ends:
+            weigh(end)
+        divide_on_scalar(second_last, banks[0], nc.sync)
+        for end in ends:
+            mask_and_round(end)
+        invert(newest, banks[1])
+        divide_on_scalar(newest, banks[1], nc.sync)
+        for end, bank in zip(ends, banks):
+            values(end, bank)
+        for end, bank in zip(ends, banks):
+            invert(end, bank)
+        divide_on_scalar(ends[0], banks[0], nc.scalar)
+        divide_on_vector(ends[1], banks[1])

@@ -22,9 +22,11 @@ HALF = NQ // 2
 BANK = 512
 RUN = 2
 
-JOBS = ((0, 0, 2), (1, 0, 2), (2, 0, 2), (3, 0, 4), (1, 2, 2), (2, 2, 2), (0, 2, 2))
-ROUNDS = ((0, 1, 2, 3), (4, 5), (6,))
+JOBS = ((0, 0, 2), (1, 0, 2), (2, 0, 2), (3, 0, 2), (1, 2, 2), (2, 2, 2), (0, 2, 2), (3, 2, 2))
+ROUNDS = ((0, 1, 2, 3, 4, 5), (6,), (7,))
 TWO_BANKS = (0, 3)
+FIRST_FILLS = 3
+K_SPLITS = (88, 48)
 EXP_LAG, SECOND_EXP_LAG = 1, 3
 
 
@@ -86,9 +88,9 @@ def tile_rows_a_exp_kb_mask_cap_kernel(tc, qT, kT, t, v, kb, mask, out):
             nc.vector.tensor_copy(out=q_bf[half][:].rearrange("p (c i j) -> p c j i", i=RUN, j=PACK),
                                   in_=q_raw[half][:].rearrange("p j (c i) -> p c j i", i=RUN))
 
-        def round_k(copy, pair):
-            copy(out=k_bf[pair][:].rearrange("p (r s j) -> p s j r", r=2, j=PACK),
-                 in_=k_raw[:].rearrange("p j (s r) -> p s j r", r=PACK)[:, :, :, 2 * pair:2 * pair + 2])
+        def round_k(copy, pair, first, stop):
+            copy(out=k_bf[pair][:].rearrange("p (r s j) -> p s j r", r=2, j=PACK)[:, first:stop],
+                 in_=k_raw[:].rearrange("p j (s r) -> p s j r", r=PACK)[:, first:stop, :, 2 * pair:2 * pair + 2])
 
         def round_v(pair):
             nc.vector.tensor_copy(out=v_bf[pair][:].rearrange("s (h c i r) -> s h c r i", h=2, i=RUN, r=PACK),
@@ -186,10 +188,12 @@ def tile_rows_a_exp_kb_mask_cap_kernel(tc, qT, kT, t, v, kb, mask, out):
         nc.scalar.activation(out=kb_scaled[:], in_=kb_sb[:], func=ACT.Copy, scale=1.0 / CAP)
         round_q(0)
         quantize(q_mx[0], q_bf[0], 0, HALF)
-        round_k(nc.vector.tensor_copy, 0)
-        round_k(nc.scalar.copy, 1)
+        round_k(nc.vector.tensor_copy, 0, 0, K_SPLITS[0])
+        round_k(nc.scalar.copy, 0, K_SPLITS[0], P)
+        round_k(nc.scalar.copy, 1, K_SPLITS[1], P)
         quantize(k_mx[0], k_bf[0], 0, P)
         quantize(k_mx[0], k_bf[0], P, 2 * P)
+        round_k(nc.vector.tensor_copy, 1, 0, K_SPLITS[1])
         quantize(k_mx[1], k_bf[1], 0, 2 * P)
         for r in range(PACK):
             nc.vector.tensor_scalar(out=mask_t[:, r, :], in0=mask_raw[:, r, :], scalar1=t_sb[:, r:r + 1],
@@ -214,8 +218,8 @@ def tile_rows_a_exp_kb_mask_cap_kernel(tc, qT, kT, t, v, kb, mask, out):
                 fills.append((job, (r, r + 1)))
         unread = {}
 
-        def fill_free_banks():
-            while fills and not unread.get(score_bank(fills[0][0], fills[0][1][0])):
+        def fill_next_bank():
+            if fills and not unread.get(score_bank(fills[0][0], fills[0][1][0])):
                 job, places = fills.pop(0)
                 unread[score_bank(job, places[0])] = len(places)
                 for r in places:
@@ -225,34 +229,36 @@ def tile_rows_a_exp_kb_mask_cap_kernel(tc, qT, kT, t, v, kb, mask, out):
             for job, r in caps[first:stop]:
                 cap(job, r)
                 unread[score_bank(job, r)] -= 1
-                fill_free_banks()
+                fill_next_bank()
 
         last_job = len(JOBS) - 1
         chunks = [(job, a, a + 2) for job in range(last_job) for a in range(0, JOBS[job][2], 2)]
-        exp_at = [caps.index((job, PACK - 1)) + 1 + EXP_LAG + (SECOND_EXP_LAG if a else 0) for job, a, b in chunks]
+        exp_at = [caps.index((job, PACK - 1)) + 1 + EXP_LAG + (1 if job == 3 else 0) for job, a, b in chunks]
         exp_at.append(len(caps))
 
-        fill_free_banks()
+        for n in range(FIRST_FILLS):
+            fill_next_bank()
         run_caps(0, exp_at[0])
         for n, chunk in enumerate(chunks):
             weigh(chunk)
             run_caps(exp_at[n], exp_at[n + 1])
+            if n >= 2:
+                invert(chunks[n - 2], y_banks[n % 2])
             mask_and_round(chunk)
-            if n == 0:
+            if n >= 2:
+                divide_on_vector(chunks[n - 2], y_banks[n % 2])
+            elif n == 0:
                 round_v(1)
-                values(chunk, y_banks[0])
-                quantize(v_mx[1], v_bf[1], 0, 2 * E)
             else:
-                invert(chunks[n - 1], y_banks[(n - 1) % 2])
-                values(chunk, y_banks[n % 2])
-                if n + 1 < len(chunks):
-                    divide_on_vector(chunks[n - 1], y_banks[(n - 1) % 2])
+                quantize(v_mx[1], v_bf[1], 0, 2 * E)
+            values(chunk, y_banks[n % 2])
 
         second_last, newest = chunks[-2], chunks[-1]
         banks = [y_banks[len(chunks) % 2], y_banks[(len(chunks) + 1) % 2]]
         ends = [(last_job, g, g + 1) for g in range(2)]
         for end in ends:
             weigh(end)
+        invert(second_last, banks[0])
         divide_on_scalar(second_last, banks[0], nc.sync)
         for end in ends:
             mask_and_round(end)
@@ -262,5 +268,5 @@ def tile_rows_a_exp_kb_mask_cap_kernel(tc, qT, kT, t, v, kb, mask, out):
             values(end, bank)
         for end, bank in zip(ends, banks):
             invert(end, bank)
-        divide_on_scalar(ends[0], banks[0], nc.scalar)
-        divide_on_vector(ends[1], banks[1])
+        for end, bank in zip(ends, banks):
+            divide_on_scalar(end, bank, nc.sync)

@@ -22,12 +22,12 @@ HALF = NQ // 2
 BANK = 512
 RUN = 2
 
-JOBS = ((0, 0, 2), (1, 0, 2), (2, 0, 2), (3, 0, 2), (1, 2, 2), (2, 2, 2), (0, 2, 2), (3, 2, 2))
+JOBS = ((0, 0), (1, 0), (2, 0), (3, 0), (1, 1), (2, 1), (0, 1), (3, 1))
+LAST_JOB = len(JOBS) - 1
+TILES = HALF // QT
 ROUNDS = ((0, 1, 2, 3, 4, 5), (6,), (7,))
 TWO_BANKS = (0, 3)
-FIRST_FILLS = 3
 K_SPLITS = (88, 48)
-EXP_LAG, SECOND_EXP_LAG = 1, 3
 
 
 def tile_rows_a_exp_kb_mask_cap_kernel(tc, qT, kT, t, v, kb, mask, out):
@@ -46,14 +46,16 @@ def tile_rows_a_exp_kb_mask_cap_kernel(tc, qT, kT, t, v, kb, mask, out):
         v_view = v.rearrange("h (s r) e -> s h (r e)", r=PACK)
         q_raw = [sb.tile([P, PACK, HALF], F32, name="q_raw%d" % half) for half in range(2)]
         k_raw = sb.tile([P, PACK, N], F32, name="k_raw")
-        mask_raw = sb.tile([P, PACK, NQ], F32, name="mask_raw")
-        v_raw = [sb.tile([P, 2, PACK * E], F32, name="v_raw%d" % pair) for pair in range(2)]
+        mask_view = mask.rearrange("(s r) q -> s r q", r=PACK)
+        mask_raw = [sb.tile([P, PACK, HALF], F32, name="mask_raw%d" % half) for half in range(2)]
+        v_raw = [sb.tile([P, 2, PACK * E], F32, name="v_raw%d" % heads) for heads in range(2)]
         nc.sync.dma_start(out=q_raw[0][:], in_=q_view[:, :, 0:HALF])
         nc.sync.dma_start(out=k_raw[:], in_=kT.rearrange("h (p j) n -> (h p) j n", j=PACK))
-        nc.sync.dma_start(out=mask_raw[:], in_=mask.rearrange("(s r) q -> s r q", r=PACK))
+        nc.sync.dma_start(out=mask_raw[0][:], in_=mask_view[:, :, 0:HALF])
         nc.sync.dma_start(out=q_raw[1][:], in_=q_view[:, :, HALF:NQ])
-        for pair in range(2):
-            nc.sync.dma_start(out=v_raw[pair][:], in_=v_view[:, 2 * pair:2 * pair + 2, :])
+        for heads in range(2):
+            nc.sync.dma_start(out=v_raw[heads][:], in_=v_view[:, 2 * heads:2 * heads + 2, :])
+        nc.sync.dma_start(out=mask_raw[1][:], in_=mask_view[:, :, HALF:NQ])
 
         def rounded(name, words):
             return sb.tile([P, PACK * words], BF16, name=name + "_bf", align_bytes=64)
@@ -72,63 +74,66 @@ def tile_rows_a_exp_kb_mask_cap_kernel(tc, qT, kT, t, v, kb, mask, out):
         q_mx = [operand("q%d" % half, HALF) for half in range(2)]
         k_bf = [rounded("k%d" % pair, 2 * P) for pair in range(2)]
         k_mx = [operand("k%d" % pair, 2 * P) for pair in range(2)]
-        v_bf = [rounded("v%d" % pair, 2 * E) for pair in range(2)]
-        v_mx = [operand("v%d" % pair, 2 * E) for pair in range(2)]
+        v_bf = [rounded("v%d" % heads, 2 * E) for heads in range(2)]
+        v_mx = [operand("v%d" % heads, 2 * E) for heads in range(2)]
         kb_scaled = sb.tile([P, PACK], F32, name="kb_scaled")
-        mask_t = sb.tile([P, PACK, NQ], F32, name="mask_t")
-        capped = [sb.tile([P, PACK, QT * job[2]], F32, name="capped%d" % n) for n, job in enumerate(JOBS)]
+        mask_t = [sb.tile([P, PACK, HALF], F32, name="mask_t%d" % half) for half in range(2)]
+        capped = [sb.tile([P, PACK, HALF], F32, name="capped%d" % job) for job in range(len(JOBS))]
 
         score_banks = {}
         for h in range(H):
-            for b in range(2 if h in TWO_BANKS else 1):
-                score_banks[h, b] = ps.tile([P, BANK], F32, name="s_%d_%d" % (h, b))
-        y_banks = [ps.tile([P, 2, E], F32, name="y%d" % b) for b in range(2)]
+            for nth in range(2 if h in TWO_BANKS else 1):
+                score_banks[h, nth] = ps.tile([P, BANK], F32, name="s_%d_%d" % (h, nth))
+        y_banks = [ps.tile([P, TILES, E], F32, name="y%d" % nth) for nth in range(2)]
 
         def round_q(half):
             nc.vector.tensor_copy(out=q_bf[half][:].rearrange("p (c i j) -> p c j i", i=RUN, j=PACK),
                                   in_=q_raw[half][:].rearrange("p j (c i) -> p c j i", i=RUN))
 
         def round_k(copy, pair, first, stop):
-            copy(out=k_bf[pair][:].rearrange("p (r s j) -> p s j r", r=2, j=PACK)[:, first:stop],
+            copy(out=k_bf[pair][:].rearrange("p (u s j) -> p s j u", u=2, j=PACK)[:, first:stop],
                  in_=k_raw[:].rearrange("p j (s r) -> p s j r", r=PACK)[:, first:stop, :, 2 * pair:2 * pair + 2])
 
-        def round_v(pair):
-            nc.vector.tensor_copy(out=v_bf[pair][:].rearrange("s (h c i r) -> s h c r i", h=2, i=RUN, r=PACK),
-                                  in_=v_raw[pair][:].rearrange("s h (r c i) -> s h c r i", r=PACK, i=RUN))
+        def round_v(heads):
+            nc.vector.tensor_copy(out=v_bf[heads][:].rearrange("s (h c i r) -> s h c r i", h=2, i=RUN, r=PACK),
+                                  in_=v_raw[heads][:].rearrange("s h (r c i) -> s h c r i", r=PACK, i=RUN))
 
-        def bank_a_place(job):
-            return job == 0 or QT * JOBS[job][2] == BANK
+        def scale_mask(half):
+            for r in range(PACK):
+                nc.vector.tensor_scalar(out=mask_t[half][:, r, :], in0=mask_raw[half][:, r, :],
+                                        scalar1=t_sb[:, r:r + 1], scalar2=None, op0=ALU.mult)
 
         def score_bank(job, r):
             h = JOBS[job][0]
-            if bank_a_place(job):
+            if job == 0:
                 return h, r % 2
             return h, r // 2 if h in TWO_BANKS else 0
 
         def score_view(job, r):
-            width = QT * JOBS[job][2]
-            first = 0 if bank_a_place(job) else width * (r % 2)
-            return score_banks[score_bank(job, r)][:, first:first + width]
+            first = 0 if job == 0 else HALF * (r % 2)
+            return score_banks[score_bank(job, r)][:, first:first + HALF]
 
         def scores(job, r):
-            h, first_tile, tiles = JOBS[job]
+            h, half = JOBS[job]
             rows = slice(ROWS * h, ROWS * (h + 1))
             k_codes, k_scales = k_mx[r // 2]
+            q_codes, q_scales = q_mx[half]
             tokens = slice(P * (r % 2), P * (r % 2 + 1))
-            for g in range(tiles):
-                half, tile_in_half = divmod(first_tile + g, 2)
-                q_codes, q_scales = q_mx[half]
-                queries = slice(QT * tile_in_half, QT * (tile_in_half + 1))
-                nc.tensor.matmul_mx(out=score_view(job, r)[:, QT * g:QT * (g + 1)],
+            for g in range(TILES):
+                queries = slice(QT * g, QT * (g + 1))
+                nc.tensor.matmul_mx(out=score_view(job, r)[:, queries],
                                     lhsT=k_codes[rows, tokens].bitcast(FP8X4), lhsT_scale=k_scales[rows, tokens],
                                     rhs=q_codes[rows, queries].bitcast(FP8X4), rhs_scale=q_scales[rows, queries],
                                     start=True, stop=True)
 
         def cap(job, r):
-            nc.scalar.activation(out=capped[job][:, r, :], in_=score_view(job, r), func=ACT.Tanh,
-                                 bias=kb_scaled[:, r:r + 1], scale=1.0 / CAP)
+            step = QT if (job, r) == (LAST_JOB, PACK - 1) else HALF
+            for first in range(0, HALF, step):
+                nc.scalar.activation(out=capped[job][:, r, first:first + step],
+                                     in_=score_view(job, r)[:, first:first + step], func=ACT.Tanh,
+                                     bias=kb_scaled[:, r:r + 1], scale=1.0 / CAP)
 
-        weights, w_bf, w_mx, inverse = {}, {}, {}, {}
+        weights, w_bf = {}, {}
 
         def weigh(chunk):
             job, a, b = chunk
@@ -137,53 +142,52 @@ def tile_rows_a_exp_kb_mask_cap_kernel(tc, qT, kT, t, v, kb, mask, out):
 
         def mask_and_round(chunk):
             job, a, b = chunk
-            first_tile = JOBS[job][1]
-            factors = mask_t[:, :, QT * (first_tile + a):QT * (first_tile + b)]
+            factors = mask_t[JOBS[job][1]][:, :, QT * a:QT * b]
             w_bf[chunk] = rounded("w%d_%d" % (job, a), QT * (b - a))
             nc.vector.tensor_tensor(out=w_bf[chunk][:].rearrange("s (c i r) -> s c r i", i=RUN, r=PACK),
                                     in0=weights[chunk][:].rearrange("s r (c i) -> s c r i", i=RUN),
                                     in1=factors.rearrange("s r (c i) -> s c r i", i=RUN), op=ALU.mult)
 
-        def values(chunk, bank):
+        def values(chunk, y):
             job, a, b = chunk
-            w_mx[chunk] = operand("w%d_%d" % (job, a), QT * (b - a))
-            quantize(w_mx[chunk], w_bf[chunk], 0, QT * (b - a))
-            pair, head_in_pair = divmod(JOBS[job][0], 2)
-            w_codes, w_scales = w_mx[chunk]
-            v_codes, v_scales = v_mx[pair]
-            features = slice(E * head_in_pair, E * (head_in_pair + 1))
+            w_mx = operand("w%d_%d" % (job, a), QT * (b - a))
+            quantize(w_mx, w_bf[chunk], 0, QT * (b - a))
+            heads, head_in_tile = divmod(JOBS[job][0], 2)
+            w_codes, w_scales = w_mx
+            v_codes, v_scales = v_mx[heads]
+            features = slice(E * head_in_tile, E * (head_in_tile + 1))
             for g in range(b - a):
                 queries = slice(QT * g, QT * (g + 1))
-                nc.tensor.matmul_mx(out=bank[:, g, :],
+                nc.tensor.matmul_mx(out=y[:, g, :],
                                     lhsT=w_codes[:, queries].bitcast(FP8X4), lhsT_scale=w_scales[:, queries],
                                     rhs=v_codes[:, features].bitcast(FP8X4), rhs_scale=v_scales[:, features],
                                     start=True, stop=True)
 
-        def invert(chunk, bank):
-            job, a, b = chunk
-            inverse[chunk] = sb.tile([P, b - a, 1], F32, name="inverse%d_%d" % (job, a))
-            nc.vector.reciprocal(out=inverse[chunk][:], in_=bank[:, 0:b - a, E - 1:E])
+        y_of = [y_banks[job % 2] for job in range(len(JOBS))]
+        inverse = [sb.tile([P, TILES, 1], F32, name="inverse%d" % job) for job in range(len(JOBS))]
 
-        def store(chunk, result, queue):
-            job, a, b = chunk
-            h, first_tile = JOBS[job][0:2]
-            rows = out[h, QT * (first_tile + a):QT * (first_tile + b), :]
-            queue.dma_start(out=rows.rearrange("(g p) e -> p g e", p=P), in_=result[:])
+        def invert(job):
+            nc.vector.reciprocal(out=inverse[job][:], in_=y_of[job][:, :, E - 1:E])
 
-        def divide_on_vector(chunk, bank):
+        def store(chunk, result):
+            job, a, b = chunk
+            h, half = JOBS[job]
+            rows = out[h, HALF * half + QT * a:HALF * half + QT * b, :]
+            nc.sync.dma_start(out=rows.rearrange("(g p) e -> p g e", p=P), in_=result[:])
+
+        def divide_on_vector(job):
+            result = sb.tile([P, TILES, E], F32, name="result%d_0" % job)
+            nc.vector.tensor_tensor(out=result[:], in0=y_of[job][:], in1=inverse[job][:].to_broadcast([P, TILES, E]),
+                                    op=ALU.mult)
+            store((job, 0, TILES), result)
+
+        def divide_on_scalar(chunk):
             job, a, b = chunk
             result = sb.tile([P, b - a, E], F32, name="result%d_%d" % (job, a))
-            nc.vector.tensor_tensor(out=result[:], in0=bank[:, 0:b - a, :],
-                                    in1=inverse[chunk][:].to_broadcast([P, b - a, E]), op=ALU.mult)
-            store(chunk, result, nc.sync)
-
-        def divide_on_scalar(chunk, bank, queue):
-            job, a, b = chunk
-            result = sb.tile([P, b - a, E], F32, name="result%d_%d" % (job, a))
-            for g in range(b - a):
-                nc.scalar.activation(out=result[:, g, :], in_=bank[:, g, :], func=ACT.Copy,
-                                     scale=inverse[chunk][:, g, :])
-            store(chunk, result, queue)
+            for g in range(a, b):
+                nc.scalar.activation(out=result[:, g - a, :], in_=y_of[job][:, g, :], func=ACT.Copy,
+                                     scale=inverse[job][:, g, :])
+            store(chunk, result)
 
         nc.scalar.activation(out=kb_scaled[:], in_=kb_sb[:], func=ACT.Copy, scale=1.0 / CAP)
         round_q(0)
@@ -195,13 +199,10 @@ def tile_rows_a_exp_kb_mask_cap_kernel(tc, qT, kT, t, v, kb, mask, out):
         quantize(k_mx[0], k_bf[0], P, 2 * P)
         round_k(nc.vector.tensor_copy, 1, 0, K_SPLITS[1])
         quantize(k_mx[1], k_bf[1], 0, 2 * P)
-        for r in range(PACK):
-            nc.vector.tensor_scalar(out=mask_t[:, r, :], in0=mask_raw[:, r, :], scalar1=t_sb[:, r:r + 1],
-                                    scalar2=None, op0=ALU.mult)
+        scale_mask(0)
         round_q(1)
         quantize(q_mx[1], q_bf[1], 0, HALF)
         round_v(0)
-        quantize(v_mx[0], v_bf[0], 0, 2 * E)
 
         caps = []
         for jobs in ROUNDS:
@@ -212,7 +213,7 @@ def tile_rows_a_exp_kb_mask_cap_kernel(tc, qT, kT, t, v, kb, mask, out):
 
         fills = []
         for job, r in caps:
-            if bank_a_place(job):
+            if job == 0:
                 fills.append((job, (r,)))
             elif r % 2 == 0:
                 fills.append((job, (r, r + 1)))
@@ -231,42 +232,46 @@ def tile_rows_a_exp_kb_mask_cap_kernel(tc, qT, kT, t, v, kb, mask, out):
                 unread[score_bank(job, r)] -= 1
                 fill_next_bank()
 
-        last_job = len(JOBS) - 1
-        chunks = [(job, a, a + 2) for job in range(last_job) for a in range(0, JOBS[job][2], 2)]
-        exp_at = [caps.index((job, PACK - 1)) + 1 + EXP_LAG + (1 if job == 3 else 0) for job, a, b in chunks]
-        exp_at.append(len(caps))
+        exp_at = [caps.index((job, PACK - 1)) + 2 for job in range(LAST_JOB)] + [len(caps)]
+        uncovered = caps.index((ROUNDS[0][-1], 1))
+        exp_at = [at + 1 if at == uncovered else at for at in exp_at]
 
-        for n in range(FIRST_FILLS):
+        for first_fill in range(3):
             fill_next_bank()
         run_caps(0, exp_at[0])
-        for n, chunk in enumerate(chunks):
+
+        for n in range(LAST_JOB):
+            chunk = (n, 0, TILES)
+            steps_left = LAST_JOB - 1 - n
             weigh(chunk)
             run_caps(exp_at[n], exp_at[n + 1])
-            if n >= 2:
-                invert(chunks[n - 2], y_banks[n % 2])
+            if n >= 2 and steps_left:
+                invert(n - 2)
             mask_and_round(chunk)
-            if n >= 2:
-                divide_on_vector(chunks[n - 2], y_banks[n % 2])
-            elif n == 0:
+            if n < 2:
+                quantize(v_mx[n], v_bf[n], 0, 2 * E)
+            elif steps_left:
+                divide_on_vector(n - 2)
+            if steps_left <= 1:
+                invert(n - 1)
+            values(chunk, y_of[n])
+            if steps_left == 1:
+                divide_on_vector(n - 1)
+            if n == 0:
                 round_v(1)
-            else:
-                quantize(v_mx[1], v_bf[1], 0, 2 * E)
-            values(chunk, y_banks[n % 2])
+            elif n == 1:
+                scale_mask(1)
 
-        second_last, newest = chunks[-2], chunks[-1]
-        banks = [y_banks[len(chunks) % 2], y_banks[(len(chunks) + 1) % 2]]
-        ends = [(last_job, g, g + 1) for g in range(2)]
-        for end in ends:
-            weigh(end)
-        invert(second_last, banks[0])
-        divide_on_scalar(second_last, banks[0], nc.sync)
-        for end in ends:
-            mask_and_round(end)
-        invert(newest, banks[1])
-        divide_on_scalar(newest, banks[1], nc.sync)
-        for end, bank in zip(ends, banks):
-            values(end, bank)
-        for end, bank in zip(ends, banks):
-            invert(end, bank)
-        for end, bank in zip(ends, banks):
-            divide_on_scalar(end, bank, nc.sync)
+        tiles = [(LAST_JOB, g, g + 1) for g in range(TILES)]
+        for chunk in tiles:
+            weigh(chunk)
+        divide_on_scalar((LAST_JOB - 2, 0, TILES))
+        for chunk in tiles:
+            mask_and_round(chunk)
+        invert(LAST_JOB - 1)
+        divide_on_scalar((LAST_JOB - 1, 0, TILES))
+        for g, chunk in enumerate(tiles):
+            values(chunk, y_of[LAST_JOB][:, g:g + 1, :])
+        invert(LAST_JOB)
+        for chunk in tiles:
+            divide_on_scalar(chunk)

from contextlib import ExitStack

import concourse.mybir as mybir

H, D, NQ, N, E = 4, 128, 512, 512, 128
CAP = 2.0
FLOPS = 2 * H * N * NQ * D + 2 * H * NQ * N * E

F32 = mybir.dt.float32
BF16 = mybir.dt.bfloat16
U32 = mybir.dt.uint32
U8 = mybir.dt.uint8
FP8X4 = mybir.dt.float8_e4m3fn_x4
ACT = mybir.ActivationFunctionType
ALU = mybir.AluOpType

P = 128
PACK = 4
ROWS = D // PACK
QT = 128
HALF = NQ // 2
BANK = 512
RUN = 2

JOBS = ((0, 0), (1, 0), (2, 0), (3, 0), (1, 1), (2, 1), (0, 1), (3, 1))
LAST_JOB = len(JOBS) - 1
TILES = HALF // QT
ROUNDS = ((0, 1, 2, 3, 4, 5), (6,), (7,))
TWO_BANKS = (0, 3)
K_SPLITS = (88, 48)


def tile_rows_a_exp_kb_mask_cap_kernel(tc, qT, kT, t, v, kb, mask, out):
    nc = tc.nc
    with ExitStack() as ctx:
        sb = ctx.enter_context(tc.tile_pool(name="sb", bufs=1))
        ps = ctx.enter_context(tc.psum_pool(name="ps", bufs=1))
        ctx.enter_context(tc.manual_schedule())

        kb_sb = sb.tile([P, PACK], F32, name="kb_sb")
        t_sb = sb.tile([P, PACK], F32, name="t_sb")
        nc.scalar.dma_start(out=kb_sb[:], in_=kb.rearrange("(s r) o -> s (r o)", r=PACK))
        nc.scalar.dma_start(out=t_sb[:], in_=t.rearrange("(s r) o -> s (r o)", r=PACK))

        q_view = qT.rearrange("h (p j) q -> (h p) j q", j=PACK)
        v_view = v.rearrange("h (s r) e -> s h (r e)", r=PACK)
        q_raw = [sb.tile([P, PACK, HALF], F32, name="q_raw%d" % half) for half in range(2)]
        k_raw = sb.tile([P, PACK, N], F32, name="k_raw")
        mask_view = mask.rearrange("(s r) q -> s r q", r=PACK)
        mask_raw = [sb.tile([P, PACK, HALF], F32, name="mask_raw%d" % half) for half in range(2)]
        v_raw = [sb.tile([P, 2, PACK * E], F32, name="v_raw%d" % heads) for heads in range(2)]
        nc.sync.dma_start(out=q_raw[0][:], in_=q_view[:, :, 0:HALF])
        nc.sync.dma_start(out=k_raw[:], in_=kT.rearrange("h (p j) n -> (h p) j n", j=PACK))
        nc.sync.dma_start(out=mask_raw[0][:], in_=mask_view[:, :, 0:HALF])
        nc.sync.dma_start(out=q_raw[1][:], in_=q_view[:, :, HALF:NQ])
        for heads in range(2):
            nc.sync.dma_start(out=v_raw[heads][:], in_=v_view[:, 2 * heads:2 * heads + 2, :])
        nc.sync.dma_start(out=mask_raw[1][:], in_=mask_view[:, :, HALF:NQ])

        def rounded(name, words):
            return sb.tile([P, PACK * words], BF16, name=name + "_bf", align_bytes=64)

        def operand(name, words):
            codes = sb.tile([P, words], U32, name=name + "_codes", align_bytes=64)
            scales = sb.tile([P, words], U8, name=name + "_scales", align_bytes=64)
            return codes, scales

        def quantize(dst, src, first, stop):
            codes, scales = dst
            nc.vector.quantize_mx(out=codes[:, first:stop].bitcast(FP8X4), scales=scales[:, first:stop],
                                  in_=src[:, PACK * first:PACK * stop])

        q_bf = [rounded("q%d" % half, HALF) for half in range(2)]
        q_mx = [operand("q%d" % half, HALF) for half in range(2)]
        k_bf = [rounded("k%d" % pair, 2 * P) for pair in range(2)]
        k_mx = [operand("k%d" % pair, 2 * P) for pair in range(2)]
        v_bf = [rounded("v%d" % heads, 2 * E) for heads in range(2)]
        v_mx = [operand("v%d" % heads, 2 * E) for heads in range(2)]
        kb_scaled = sb.tile([P, PACK], F32, name="kb_scaled")
        mask_t = [sb.tile([P, PACK, HALF], F32, name="mask_t%d" % half) for half in range(2)]
        capped = [sb.tile([P, PACK, HALF], F32, name="capped%d" % job) for job in range(len(JOBS))]

        score_banks = {}
        for h in range(H):
            for nth in range(2 if h in TWO_BANKS else 1):
                score_banks[h, nth] = ps.tile([P, BANK], F32, name="s_%d_%d" % (h, nth))
        y_banks = [ps.tile([P, TILES, E], F32, name="y%d" % nth) for nth in range(2)]

        def round_q(half):
            nc.vector.tensor_copy(out=q_bf[half][:].rearrange("p (c i j) -> p c j i", i=RUN, j=PACK),
                                  in_=q_raw[half][:].rearrange("p j (c i) -> p c j i", i=RUN))

        def round_k(copy, pair, first, stop):
            copy(out=k_bf[pair][:].rearrange("p (u s j) -> p s j u", u=2, j=PACK)[:, first:stop],
                 in_=k_raw[:].rearrange("p j (s r) -> p s j r", r=PACK)[:, first:stop, :, 2 * pair:2 * pair + 2])

        def round_v(heads):
            nc.vector.tensor_copy(out=v_bf[heads][:].rearrange("s (h c i r) -> s h c r i", h=2, i=RUN, r=PACK),
                                  in_=v_raw[heads][:].rearrange("s h (r c i) -> s h c r i", r=PACK, i=RUN))

        def scale_mask(half):
            for r in range(PACK):
                nc.vector.tensor_scalar(out=mask_t[half][:, r, :], in0=mask_raw[half][:, r, :],
                                        scalar1=t_sb[:, r:r + 1], scalar2=None, op0=ALU.mult)

        def score_bank(job, r):
            h = JOBS[job][0]
            if job == 0:
                return h, r % 2
            return h, r // 2 if h in TWO_BANKS else 0

        def score_view(job, r):
            first = 0 if job == 0 else HALF * (r % 2)
            return score_banks[score_bank(job, r)][:, first:first + HALF]

        def scores(job, r):
            h, half = JOBS[job]
            rows = slice(ROWS * h, ROWS * (h + 1))
            k_codes, k_scales = k_mx[r // 2]
            q_codes, q_scales = q_mx[half]
            tokens = slice(P * (r % 2), P * (r % 2 + 1))
            for g in range(TILES):
                queries = slice(QT * g, QT * (g + 1))
                nc.tensor.matmul_mx(out=score_view(job, r)[:, queries],
                                    lhsT=k_codes[rows, tokens].bitcast(FP8X4), lhsT_scale=k_scales[rows, tokens],
                                    rhs=q_codes[rows, queries].bitcast(FP8X4), rhs_scale=q_scales[rows, queries],
                                    start=True, stop=True)

        def cap(job, r):
            step = QT if (job, r) == (LAST_JOB, PACK - 1) else HALF
            for first in range(0, HALF, step):
                nc.scalar.activation(out=capped[job][:, r, first:first + step],
                                     in_=score_view(job, r)[:, first:first + step], func=ACT.Tanh,
                                     bias=kb_scaled[:, r:r + 1], scale=1.0 / CAP)

        weights, w_bf = {}, {}

        def weigh(chunk):
            job, a, b = chunk
            weights[chunk] = sb.tile([P, PACK, QT * (b - a)], F32, name="weights%d_%d" % (job, a))
            nc.scalar.activation(out=weights[chunk][:], in_=capped[job][:, :, QT * a:QT * b], func=ACT.Exp, scale=CAP)

        def mask_and_round(chunk):
            job, a, b = chunk
            factors = mask_t[JOBS[job][1]][:, :, QT * a:QT * b]
            w_bf[chunk] = rounded("w%d_%d" % (job, a), QT * (b - a))
            nc.vector.tensor_tensor(out=w_bf[chunk][:].rearrange("s (c i r) -> s c r i", i=RUN, r=PACK),
                                    in0=weights[chunk][:].rearrange("s r (c i) -> s c r i", i=RUN),
                                    in1=factors.rearrange("s r (c i) -> s c r i", i=RUN), op=ALU.mult)

        def values(chunk, y):
            job, a, b = chunk
            w_mx = operand("w%d_%d" % (job, a), QT * (b - a))
            quantize(w_mx, w_bf[chunk], 0, QT * (b - a))
            heads, head_in_tile = divmod(JOBS[job][0], 2)
            w_codes, w_scales = w_mx
            v_codes, v_scales = v_mx[heads]
            features = slice(E * head_in_tile, E * (head_in_tile + 1))
            for g in range(b - a):
                queries = slice(QT * g, QT * (g + 1))
                nc.tensor.matmul_mx(out=y[:, g, :],
                                    lhsT=w_codes[:, queries].bitcast(FP8X4), lhsT_scale=w_scales[:, queries],
                                    rhs=v_codes[:, features].bitcast(FP8X4), rhs_scale=v_scales[:, features],
                                    start=True, stop=True)

        y_of = [y_banks[job % 2] for job in range(len(JOBS))]
        inverse = [sb.tile([P, TILES, 1], F32, name="inverse%d" % job) for job in range(len(JOBS))]

        def invert(job):
            nc.vector.reciprocal(out=inverse[job][:], in_=y_of[job][:, :, E - 1:E])

        def store(chunk, result):
            job, a, b = chunk
            h, half = JOBS[job]
            rows = out[h, HALF * half + QT * a:HALF * half + QT * b, :]
            nc.sync.dma_start(out=rows.rearrange("(g p) e -> p g e", p=P), in_=result[:])

        def divide_on_vector(job):
            result = sb.tile([P, TILES, E], F32, name="result%d_0" % job)
            nc.vector.tensor_tensor(out=result[:], in0=y_of[job][:], in1=inverse[job][:].to_broadcast([P, TILES, E]),
                                    op=ALU.mult)
            store((job, 0, TILES), result)

        def divide_on_scalar(chunk):
            job, a, b = chunk
            result = sb.tile([P, b - a, E], F32, name="result%d_%d" % (job, a))
            for g in range(a, b):
                nc.scalar.activation(out=result[:, g - a, :], in_=y_of[job][:, g, :], func=ACT.Copy,
                                     scale=inverse[job][:, g, :])
            store(chunk, result)

        nc.scalar.activation(out=kb_scaled[:], in_=kb_sb[:], func=ACT.Copy, scale=1.0 / CAP)
        round_q(0)
        quantize(q_mx[0], q_bf[0], 0, HALF)
        round_k(nc.vector.tensor_copy, 0, 0, K_SPLITS[0])
        round_k(nc.scalar.copy, 0, K_SPLITS[0], P)
        round_k(nc.scalar.copy, 1, K_SPLITS[1], P)
        quantize(k_mx[0], k_bf[0], 0, P)
        quantize(k_mx[0], k_bf[0], P, 2 * P)
        round_k(nc.vector.tensor_copy, 1, 0, K_SPLITS[1])
        quantize(k_mx[1], k_bf[1], 0, 2 * P)
        scale_mask(0)
        round_q(1)
        quantize(q_mx[1], q_bf[1], 0, HALF)
        round_v(0)

        caps = []
        for jobs in ROUNDS:
            caps.extend([(jobs[0], 0), (jobs[0], 1)])
            for before, job in zip(jobs, jobs[1:]):
                caps.extend([(job, 0), (job, 1), (before, 2), (before, 3)])
            caps.extend([(jobs[-1], 2), (jobs[-1], 3)])

        fills = []
        for job, r in caps:
            if job == 0:
                fills.append((job, (r,)))
            elif r % 2 == 0:
                fills.append((job, (r, r + 1)))
        unread = {}

        def fill_next_bank():
            if fills and not unread.get(score_bank(fills[0][0], fills[0][1][0])):
                job, places = fills.pop(0)
                unread[score_bank(job, places[0])] = len(places)
                for r in places:
                    scores(job, r)

        def run_caps(first, stop):
            for job, r in caps[first:stop]:
                cap(job, r)
                unread[score_bank(job, r)] -= 1
                fill_next_bank()

        exp_at = [caps.index((job, PACK - 1)) + 2 for job in range(LAST_JOB)] + [len(caps)]
        uncovered = caps.index((ROUNDS[0][-1], 1))
        exp_at = [at + 1 if at == uncovered else at for at in exp_at]

        for first_fill in range(3):
            fill_next_bank()
        run_caps(0, exp_at[0])

        for n in range(LAST_JOB):
            chunk = (n, 0, TILES)
            steps_left = LAST_JOB - 1 - n
            weigh(chunk)
            run_caps(exp_at[n], exp_at[n + 1])
            if n >= 2 and steps_left:
                invert(n - 2)
            mask_and_round(chunk)
            if n < 2:
                quantize(v_mx[n], v_bf[n], 0, 2 * E)
            elif steps_left:
                divide_on_vector(n - 2)
            if steps_left <= 1:
                invert(n - 1)
            values(chunk, y_of[n])
            if steps_left == 1:
                divide_on_vector(n - 1)
            if n == 0:
                round_v(1)
            elif n == 1:
                scale_mask(1)

        tiles = [(LAST_JOB, g, g + 1) for g in range(TILES)]
        for chunk in tiles:
            weigh(chunk)
        divide_on_scalar((LAST_JOB - 2, 0, TILES))
        for chunk in tiles:
            mask_and_round(chunk)
        invert(LAST_JOB - 1)
        divide_on_scalar((LAST_JOB - 1, 0, TILES))
        for g, chunk in enumerate(tiles):
            values(chunk, y_of[LAST_JOB][:, g:g + 1, :])
        invert(LAST_JOB)
        for chunk in tiles:
            divide_on_scalar(chunk)
